import numpy as np
import ml_dtypes


def mxq(x, axis, fmt="e4m3"):
    dtype, down = {"e4m3": (ml_dtypes.float8_e4m3fn, 7), "e5m2": (ml_dtypes.float8_e5m2, 14)}[fmt]
    v = np.moveaxis(np.asarray(x, np.float32).astype(ml_dtypes.bfloat16).astype(np.float64), axis, -1)
    blocks = v.reshape(v.shape[:-1] + (-1, 32))
    amax = np.abs(blocks).max(-1, keepdims=True)
    byte = np.maximum(np.where(amax > 0, np.frexp(amax)[1] - 1 + 127, 0) - down, 1)
    scale = np.exp2(byte - 127.0)
    codes = (blocks / scale).astype(np.float32).astype(dtype).astype(np.float64)
    return np.moveaxis((codes * scale).reshape(v.shape), -1, axis)


WIDE = False


def mx_kscale(k):
    if not WIDE:
        return np.ones(k)
    levels = np.array([10, -10, 5, -5, 0])
    if k % 512:
        return np.exp2(np.random.permutation(np.resize(levels, k // 32))).repeat(32)
    a = np.empty((k // 512, 16))
    for p in range(k // 512):
        a[p, :8] = np.random.permutation(np.resize(levels, 8))
        for g in range(8):
            far = levels[np.abs(levels - a[p, g]) >= 10]
            a[p, g + 8] = far[np.random.randint(len(far))]
    return np.exp2(a.ravel()).repeat(32)


def f64(x):
    return np.asarray(x).astype(np.float64)


def striped(idx):
    return np.tile(np.asarray(idx).reshape(-1, 16).T, (8, 1)).astype(np.uint16)


def unstriped(offs):
    return offs[:16].T.reshape(-1).astype(np.int64)


E2M1 = np.array([0.0, 0.5, 1.0, 1.5, 2.0, 3.0, 4.0, 6.0, -0.0, -0.5, -1.0, -1.5, -2.0, -3.0, -4.0, -6.0])


def pack_weight(w, fmt):
    k, n = w.shape
    w = f64(np.asarray(w, np.float32).astype(ml_dtypes.bfloat16)).reshape(k // 32, 32, n)
    amax = np.abs(w).max(1)
    if fmt == "e4m3":
        byte = np.frexp(amax)[1] - 1 + 127 - 7
    else:
        mant, ex = np.frexp(amax / 6.0)
        byte = np.where(mant > 0.5, ex, ex - 1) + 127
    byte = np.clip(np.where(amax > 0, byte, 1), 1, 254)
    scaled = (w * np.exp2(127.0 - byte)[:, None, :]).reshape(k, n).astype(np.float32)
    by_word = np.ascontiguousarray(scaled.reshape(k // 512, 128, 4, n).transpose(0, 1, 3, 2))
    if fmt == "e4m3":
        words = by_word.astype(ml_dtypes.float8_e4m3fn).view(np.uint8)
    else:
        c = by_word.astype(ml_dtypes.float4_e2m1fn).view(np.uint8) & 0xF
        words = (c[..., 0::2] | (c[..., 1::2] << 4)).reshape(k // 512, 128, 2 * n)
    return np.ascontiguousarray(words), np.ascontiguousarray(byte.astype(np.uint8).reshape(k // 512, 16, n))


def unpack_weight(words, scales, fmt):
    g, _, n = scales.shape
    words = np.ascontiguousarray(words).reshape(g, 128, n, -1)
    if fmt == "e4m3":
        vals = words.view(ml_dtypes.float8_e4m3fn).astype(np.float64)
    else:
        nib = np.empty((g, 128, n, 4), np.uint8)
        nib[..., 0::2] = words & 0xF
        nib[..., 1::2] = words >> 4
        vals = E2M1[nib]
    vals = vals * np.repeat(np.exp2(scales.astype(np.float64) - 127.0), 8, axis=1)[..., None]
    return vals.transpose(0, 1, 3, 2).reshape(g * 512, n)


K, T, J, N = 512, 512, 512, 512


def setup_inputs():
    n = np.random.standard_normal
    idx = np.random.randint(0, T, J)
    idx2 = np.random.randint(0, T, J)
    idx3 = np.random.randint(0, T, J)
    fk = mx_kscale(K)
    xtp = pack_weight(n((K, T)) / fk[:, None], "e4m3")
    wap = pack_weight(n((K, N)) * 1 / np.sqrt(K) * fk[:, None], "e2m1")
    wcp = pack_weight(n((K, N)) * 1 / np.sqrt(K) * fk[:, None], "e4m3")
    return {
        "xt_words": xtp[0],
        "xt_scales": xtp[1],
        "wa_words": wap[0],
        "wa_scales": wap[1],
        "wb": (n((K, N)) * 1 / np.sqrt(K) * fk[:, None]).astype(np.float32),
        "wc_words": wcp[0],
        "wc_scales": wcp[1],
        "offs": striped(idx),
        "offs2": striped(idx2),
        "offs3": striped(idx3),
    }


def reference(xt_words, xt_scales, wa_words, wa_scales, wb, wc_words, wc_scales, offs, offs2, offs3):
    idx = unstriped(offs)
    idx2 = unstriped(offs2)
    idx3 = unstriped(offs3)
    xtu = unpack_weight(xt_words, xt_scales, "e4m3")
    wau = unpack_weight(wa_words, wa_scales, "e2m1")
    wcu = unpack_weight(wc_words, wc_scales, "e4m3")
    za = wau.T @ xtu
    wbq = mxq(f64(wb), 0, "e4m3")
    zb = wbq.T @ xtu
    zc = wcu.T @ xtu
    lo = np.minimum(za[:, idx], zb[:, idx2])
    hi = np.maximum(za[:, idx], zb[:, idx2])
    y = np.maximum(lo, np.minimum(hi, zc[:, idx3]))
    return y

@@ -1,0 +1,171 @@
+from contextlib import ExitStack
+
+import concourse.mybir as mybir
+
+K, T, J, N = 512, 512, 512, 512
+FLOPS = 3 * 2 * K * T * N
+
+F32 = mybir.dt.float32
+BF16 = mybir.dt.bfloat16
+I32 = mybir.dt.int32
+U32 = mybir.dt.uint32
+U16 = mybir.dt.uint16
+U8 = mybir.dt.uint8
+FP8X4 = mybir.dt.float8_e4m3fn_x4
+FP4X4 = mybir.dt.float4_e2m1fn_x4
+MIN = mybir.AluOpType.min
+MAX = mybir.AluOpType.max
+
+P = 128
+PACK = 4
+TILES = N // P
+WINDOW = 704
+
+
+def tile_list_middle_of_three_kernel(
+    tc, xt_words, xt_scales, wa_words, wa_scales, wb, wc_words, wc_scales, offs, offs2, offs3, out
+):
+    nc = tc.nc
+    with ExitStack() as ctx:
+        keep = ctx.enter_context(tc.tile_pool(name="keep", bufs=1))
+        psum = ctx.enter_context(tc.psum_pool(name="psum", bufs=8))
+
+        list_a = keep.tile([P, J // 16], U16, name="list_a")
+        list_b = keep.tile([P, J // 16], U16, name="list_b")
+        list_c = keep.tile([P, J // 16], U16, name="list_c")
+        x_codes = keep.tile([P, T], U32, name="x_codes", align_bytes=64)
+        x_plane = keep.tile([P, T], U8, name="x_plane", align_bytes=64)
+        a_codes = keep.tile([P, 2 * N], U8, name="a_codes", align_bytes=64)
+        a_plane = keep.tile([P, N], U8, name="a_plane", align_bytes=64)
+        c_codes = keep.tile([P, N], U32, name="c_codes", align_bytes=64)
+        c_plane = keep.tile([P, N], U8, name="c_plane", align_bytes=64)
+
+        pieces = [(0, 128), (128, 256), (256, 512)]
+        b_raw = [keep.tile([P, PACK, e - s], F32, name="b_raw%d" % s) for s, e in pieces]
+        b_grouped = [keep.tile([P, e - s, PACK], BF16, name="b_grouped%d" % s, align_bytes=64) for s, e in pieces]
+        b_codes = [keep.tile([P, e - s], U32, name="b_codes%d" % s, align_bytes=64) for s, e in pieces]
+        b_plane = [keep.tile([P, e - s], U8, name="b_plane%d" % s, align_bytes=64) for s, e in pieces]
+
+        za = keep.tile([P, TILES, WINDOW], F32, name="za")
+        zb = keep.tile([P, TILES, WINDOW], F32, name="zb")
+        zc = keep.tile([P, TILES, WINDOW], F32, name="zc")
+        ga = [keep.tile([P, J], F32, name="ga%d" % i) for i in range(TILES)]
+        gb = [keep.tile([P, J], F32, name="gb%d" % i) for i in range(TILES)]
+        gc = [keep.tile([P, J], F32, name="gc%d" % i) for i in range(TILES)]
+        lo = [keep.tile([P, J], F32, name="lo%d" % i) for i in range(TILES)]
+        hi = [keep.tile([P, J], F32, name="hi%d" % i) for i in range(TILES)]
+        capped = [keep.tile([P, J], F32, name="capped%d" % i) for i in range(TILES)]
+        middle = [keep.tile([P, J], F32, name="middle%d" % i) for i in range(TILES)]
+
+        wb_rows = wb.rearrange("(p j) n -> p j n", j=PACK)
+
+        def load_plane(plane, scales):
+            for q in range(4):
+                nc.sync.dma_start(
+                    out=plane[32 * q : 32 * q + 4, :].bitcast(I32),
+                    in_=scales[0, 4 * q : 4 * q + 4, :].bitcast(I32),
+                )
+
+        def load_b(u):
+            s, e = pieces[u]
+            nc.sync.dma_start(out=b_raw[u][:], in_=wb_rows[:, :, s:e])
+
+        def quantize_b(u):
+            nc.vector.quantize_mx(
+                out=b_codes[u][:].bitcast(FP8X4),
+                scales=b_plane[u][:],
+                in_=b_grouped[u][:].rearrange("p n j -> p (n j)"),
+            )
+
+        def product(z, i, codes, plane):
+            bank = psum.tile([P, T], F32, name="bank")
+            nc.tensor.matmul_mx(
+                out=bank[:], lhsT=codes, lhsT_scale=plane,
+                rhs=x_codes[:].bitcast(FP8X4), rhs_scale=x_plane[:], start=True, stop=True,
+            )
+            nc.scalar.copy(out=z[:, i, 0:T], in_=bank[:])
+
+        def product_a(i):
+            product(za, i, a_codes[:, 2 * P * i : 2 * P * (i + 1)].bitcast(FP4X4), a_plane[:, P * i : P * (i + 1)])
+
+        def product_b(i):
+            u = min(i, 2)
+            s = P * i - pieces[u][0]
+            product(zb, i, b_codes[u][:, s : s + P].bitcast(FP8X4), b_plane[u][:, s : s + P])
+
+        def product_c(i):
+            product(zc, i, c_codes[:, P * i : P * (i + 1)].bitcast(FP8X4), c_plane[:, P * i : P * (i + 1)])
+
+        def gather(g, z, offsets, i):
+            nc.vector.tensor_copy(out=g[i][:], in_=z[:, i, :].indirect(offsets[:]))
+
+        def bounds(i):
+            nc.vector.tensor_tensor(out=lo[i][:], in0=ga[i][:], in1=gb[i][:], op=MIN)
+            nc.vector.tensor_tensor(out=hi[i][:], in0=ga[i][:], in1=gb[i][:], op=MAX)
+
+        def cap(i):
+            nc.vector.tensor_tensor(out=capped[i][:], in0=hi[i][:], in1=gc[i][:], op=MIN)
+
+        def finish(i):
+            nc.vector.tensor_tensor(out=middle[i][:], in0=lo[i][:], in1=capped[i][:], op=MAX)
+            nc.sync.dma_start(out=out[P * i : P * (i + 1), :], in_=middle[i][:])
+
+        for plane in (x_plane, a_plane, c_plane):
+            nc.vector.memset(plane[:].bitcast(I32), 0)
+        nc.vector.memset(zb[:, :, T:WINDOW], 0.0)
+        nc.scalar.copy(out=za[:, :, T:WINDOW], in_=zb[:, :, T:WINDOW])
+        nc.scalar.copy(out=zc[:, :, T:WINDOW], in_=zb[:, :, T:WINDOW])
+
+        load_b(0)
+        nc.sync.dma_start(out=x_codes[:].bitcast(I32), in_=xt_words[0].rearrange("p n t -> p (n t)").bitcast(I32))
+        load_plane(x_plane, xt_scales)
+        load_b(1)
+        nc.sync.dma_start(list_b[:], offs2)
+        nc.sync.dma_start(out=a_codes[:].bitcast(I32), in_=wa_words[0].bitcast(I32))
+        load_plane(a_plane, wa_scales)
+        nc.sync.dma_start(list_a[:], offs)
+        load_b(2)
+        nc.sync.dma_start(out=c_codes[:].bitcast(I32), in_=wc_words[0].rearrange("p n t -> p (n t)").bitcast(I32))
+        load_plane(c_plane, wc_scales)
+        nc.sync.dma_start(list_c[:], offs3)
+
+        nc.vector.tensor_copy(out=b_grouped[0][:], in_=b_raw[0][:].rearrange("p j n -> p n j"))
+        nc.scalar.copy(out=b_grouped[1][:], in_=b_raw[1][:].rearrange("p j n -> p n j"))
+        quantize_b(0)
+        quantize_b(1)
+        product_b(0)
+        product_b(1)
+        product_a(0)
+        product_a(1)
+        nc.scalar.copy(out=b_grouped[2][:], in_=b_raw[2][:].rearrange("p j n -> p n j"))
+        gather(gb, zb, list_b, 0)
+        gather(gb, zb, list_b, 1)
+        gather(ga, za, list_a, 0)
+        gather(ga, za, list_a, 1)
+        quantize_b(2)
+        for i in (2, 3):
+            product_a(i)
+        for i in (2, 3):
+            product_b(i)
+        for i in range(TILES):
+            product_c(i)
+        bounds(0)
+        bounds(1)
+        for i in (2, 3):
+            gather(ga, za, list_a, i)
+        for i in (2, 3):
+            gather(gb, zb, list_b, i)
+        gather(gc, zc, list_c, 0)
+        gather(gc, zc, list_c, 1)
+        bounds(2)
+        bounds(3)
+        cap(0)
+        gather(gc, zc, list_c, 2)
+        finish(0)
+        cap(1)
+        gather(gc, zc, list_c, 3)
+        finish(1)
+        cap(2)
+        cap(3)
+        finish(2)
+        finish(3)

@@ -19,7 +19,7 @@ MAX = mybir.AluOpType.max
 P = 128
 PACK = 4
 TILES = N // P
-WINDOW = 704
+SPARE = 192
 
 
 def tile_list_middle_of_three_kernel(
@@ -46,9 +46,12 @@ def tile_list_middle_of_three_kernel(
         b_codes = [keep.tile([P, e - s], U32, name="b_codes%d" % s, align_bytes=64) for s, e in pieces]
         b_plane = [keep.tile([P, e - s], U8, name="b_plane%d" % s, align_bytes=64) for s, e in pieces]
 
-        za = keep.tile([P, TILES, WINDOW], F32, name="za")
-        zb = keep.tile([P, TILES, WINDOW], F32, name="zb")
-        zc = keep.tile([P, TILES, WINDOW], F32, name="zc")
+        za = keep.tile([P, TILES * T + SPARE], F32, name="za")
+        zb = keep.tile([P, TILES * T + SPARE], F32, name="zb")
+        zc = keep.tile([P, TILES * T + SPARE], F32, name="zc")
+        place_a = [2 * T, 3 * T, 0, T]
+        place_b = [3 * T, 2 * T, 0, T]
+        place_c = [2 * T, 3 * T, 0, T]
         ga = [keep.tile([P, J], F32, name="ga%d" % i) for i in range(TILES)]
         gb = [keep.tile([P, J], F32, name="gb%d" % i) for i in range(TILES)]
         gc = [keep.tile([P, J], F32, name="gc%d" % i) for i in range(TILES)]
@@ -77,44 +80,56 @@ def tile_list_middle_of_three_kernel(
                 in_=b_grouped[u][:].rearrange("p n j -> p (n j)"),
             )
 
-        def product(z, i, codes, plane):
+        def product(z, at, codes, plane):
             bank = psum.tile([P, T], F32, name="bank")
             nc.tensor.matmul_mx(
                 out=bank[:], lhsT=codes, lhsT_scale=plane,
                 rhs=x_codes[:].bitcast(FP8X4), rhs_scale=x_plane[:], start=True, stop=True,
             )
-            nc.scalar.copy(out=z[:, i, 0:T], in_=bank[:])
+            nc.scalar.copy(out=z[:, at : at + T], in_=bank[:])
+
+        def first_product():
+            at = place_b[0]
+            half = T // 2
+            for h, copy in enumerate((nc.scalar.copy, nc.vector.tensor_copy)):
+                bank = psum.tile([P, T], F32, name="bank")
+                nc.tensor.matmul_mx(
+                    out=bank[:, 0:half], lhsT=b_codes[0][:].bitcast(FP8X4), lhsT_scale=b_plane[0][:],
+                    rhs=x_codes[:, half * h : half * (h + 1)].bitcast(FP8X4),
+                    rhs_scale=x_plane[:, half * h : half * (h + 1)], start=True, stop=True,
+                )
+                copy(out=zb[:, at + half * h : at + half * (h + 1)], in_=bank[:, 0:half])
 
         def product_a(i):
-            product(za, i, a_codes[:, 2 * P * i : 2 * P * (i + 1)].bitcast(FP4X4), a_plane[:, P * i : P * (i + 1)])
+            product(za, place_a[i], a_codes[:, 2 * P * i : 2 * P * (i + 1)].bitcast(FP4X4), a_plane[:, P * i : P * (i + 1)])
 
         def product_b(i):
             u = min(i, 2)
             s = P * i - pieces[u][0]
-            product(zb, i, b_codes[u][:, s : s + P].bitcast(FP8X4), b_plane[u][:, s : s + P])
+            product(zb, place_b[i], b_codes[u][:, s : s + P].bitcast(FP8X4), b_plane[u][:, s : s + P])
 
         def product_c(i):
-            product(zc, i, c_codes[:, P * i : P * (i + 1)].bitcast(FP8X4), c_plane[:, P * i : P * (i + 1)])
+            product(zc, place_c[i], c_codes[:, P * i : P * (i + 1)].bitcast(FP8X4), c_plane[:, P * i : P * (i + 1)])
 
-        def gather(g, z, offsets, i):
-            nc.vector.tensor_copy(out=g[i][:], in_=z[:, i, :].indirect(offsets[:]))
+        def gather(g, z, place, offsets, i):
+            nc.vector.tensor_copy(out=g[i][:], in_=z[:, place[i] : place[i] + T + SPARE].indirect(offsets[:]))
 
         def bounds(i):
             nc.vector.tensor_tensor(out=lo[i][:], in0=ga[i][:], in1=gb[i][:], op=MIN)
             nc.vector.tensor_tensor(out=hi[i][:], in0=ga[i][:], in1=gb[i][:], op=MAX)
 
-        def cap(i):
-            nc.vector.tensor_tensor(out=capped[i][:], in0=hi[i][:], in1=gc[i][:], op=MIN)
+        def cap(i, cols=slice(0, J)):
+            nc.vector.tensor_tensor(out=capped[i][:, cols], in0=hi[i][:, cols], in1=gc[i][:, cols], op=MIN)
 
-        def finish(i):
-            nc.vector.tensor_tensor(out=middle[i][:], in0=lo[i][:], in1=capped[i][:], op=MAX)
-            nc.sync.dma_start(out=out[P * i : P * (i + 1), :], in_=middle[i][:])
+        def finish(i, cols=slice(0, J), queue=nc.sync):
+            nc.vector.tensor_tensor(out=middle[i][:, cols], in0=lo[i][:, cols], in1=capped[i][:, cols], op=MAX)
+            queue.dma_start(out=out[P * i : P * (i + 1), cols], in_=middle[i][:, cols])
 
         for plane in (x_plane, a_plane, c_plane):
             nc.vector.memset(plane[:].bitcast(I32), 0)
-        nc.vector.memset(zb[:, :, T:WINDOW], 0.0)
-        nc.scalar.copy(out=za[:, :, T:WINDOW], in_=zb[:, :, T:WINDOW])
-        nc.scalar.copy(out=zc[:, :, T:WINDOW], in_=zb[:, :, T:WINDOW])
+        nc.vector.memset(zb[:, TILES * T :], 0.0)
+        nc.scalar.copy(out=za[:, TILES * T :], in_=zb[:, TILES * T :])
+        nc.scalar.copy(out=zc[:, TILES * T :], in_=zb[:, TILES * T :])
 
         load_b(0)
         nc.sync.dma_start(out=x_codes[:].bitcast(I32), in_=xt_words[0].rearrange("p n t -> p (n t)").bitcast(I32))
@@ -133,15 +148,15 @@ def tile_list_middle_of_three_kernel(
         nc.scalar.copy(out=b_grouped[1][:], in_=b_raw[1][:].rearrange("p j n -> p n j"))
         quantize_b(0)
         quantize_b(1)
-        product_b(0)
+        first_product()
         product_b(1)
         product_a(0)
         product_a(1)
         nc.scalar.copy(out=b_grouped[2][:], in_=b_raw[2][:].rearrange("p j n -> p n j"))
-        gather(gb, zb, list_b, 0)
-        gather(gb, zb, list_b, 1)
-        gather(ga, za, list_a, 0)
-        gather(ga, za, list_a, 1)
+        gather(gb, zb, place_b, list_b, 0)
+        gather(gb, zb, place_b, list_b, 1)
+        gather(ga, za, place_a, list_a, 0)
+        gather(ga, za, place_a, list_a, 1)
         quantize_b(2)
         for i in (2, 3):
             product_a(i)
@@ -152,20 +167,23 @@ def tile_list_middle_of_three_kernel(
         bounds(0)
         bounds(1)
         for i in (2, 3):
-            gather(ga, za, list_a, i)
+            gather(ga, za, place_a, list_a, i)
         for i in (2, 3):
-            gather(gb, zb, list_b, i)
-        gather(gc, zc, list_c, 0)
-        gather(gc, zc, list_c, 1)
+            gather(gb, zb, place_b, list_b, i)
         bounds(2)
         bounds(3)
+        gather(gc, zc, place_c, list_c, 0)
+        gather(gc, zc, place_c, list_c, 1)
         cap(0)
-        gather(gc, zc, list_c, 2)
+        gather(gc, zc, place_c, list_c, 2)
         finish(0)
         cap(1)
-        gather(gc, zc, list_c, 3)
-        finish(1)
         cap(2)
-        cap(3)
+        finish(1)
+        gather(gc, zc, place_c, list_c, 3)
         finish(2)
-        finish(3)
+        halves = (slice(0, J // 2), slice(J // 2, J))
+        for cols in halves:
+            cap(3, cols)
+        finish(3, halves[0], nc.scalar)
+        finish(3, halves[1], nc.sync)

@@ -62,9 +62,9 @@ def tile_list_middle_of_three_kernel(
 
         wb_rows = wb.rearrange("(p j) n -> p j n", j=PACK)
 
-        def load_plane(plane, scales):
+        def load_plane(plane, scales, queue=nc.sync):
             for q in range(4):
-                nc.sync.dma_start(
+                queue.dma_start(
                     out=plane[32 * q : 32 * q + 4, :].bitcast(I32),
                     in_=scales[0, 4 * q : 4 * q + 4, :].bitcast(I32),
                 )
@@ -128,12 +128,12 @@ def tile_list_middle_of_three_kernel(
         for plane in (x_plane, a_plane, c_plane):
             nc.vector.memset(plane[:].bitcast(I32), 0)
         nc.vector.memset(zb[:, TILES * T :], 0.0)
-        nc.scalar.copy(out=za[:, TILES * T :], in_=zb[:, TILES * T :])
-        nc.scalar.copy(out=zc[:, TILES * T :], in_=zb[:, TILES * T :])
 
         load_b(0)
         nc.sync.dma_start(out=x_codes[:].bitcast(I32), in_=xt_words[0].rearrange("p n t -> p (n t)").bitcast(I32))
-        load_plane(x_plane, xt_scales)
+        load_plane(x_plane, xt_scales, nc.scalar)
+        nc.scalar.copy(out=za[:, TILES * T :], in_=zb[:, TILES * T :])
+        nc.scalar.copy(out=zc[:, TILES * T :], in_=zb[:, TILES * T :])
         load_b(1)
         nc.sync.dma_start(list_b[:], offs2)
         nc.sync.dma_start(out=a_codes[:].bitcast(I32), in_=wa_words[0].bitcast(I32))
@@ -145,8 +145,8 @@ def tile_list_middle_of_three_kernel(
         nc.sync.dma_start(list_c[:], offs3)
 
         nc.vector.tensor_copy(out=b_grouped[0][:], in_=b_raw[0][:].rearrange("p j n -> p n j"))
-        nc.scalar.copy(out=b_grouped[1][:], in_=b_raw[1][:].rearrange("p j n -> p n j"))
         quantize_b(0)
+        nc.vector.tensor_copy(out=b_grouped[1][:], in_=b_raw[1][:].rearrange("p j n -> p n j"))
         quantize_b(1)
         first_product()
         product_b(1)

@@ -49,7 +49,7 @@ def tile_list_middle_of_three_kernel(
         za = keep.tile([P, TILES * T + SPARE], F32, name="za")
         zb = keep.tile([P, TILES * T + SPARE], F32, name="zb")
         zc = keep.tile([P, TILES * T + SPARE], F32, name="zc")
-        place_a = [2 * T, 3 * T, 0, T]
+        place_a = [3 * T, 2 * T, 0, T]
         place_b = [3 * T, 2 * T, 0, T]
         place_c = [2 * T, 3 * T, 0, T]
         ga = [keep.tile([P, J], F32, name="ga%d" % i) for i in range(TILES)]
@@ -62,8 +62,8 @@ def tile_list_middle_of_three_kernel(
 
         wb_rows = wb.rearrange("(p j) n -> p j n", j=PACK)
 
-        def load_plane(plane, scales, queue=nc.sync):
-            for q in range(4):
+        def load_plane(plane, scales, queues=(nc.sync,) * 4):
+            for q, queue in enumerate(queues):
                 queue.dma_start(
                     out=plane[32 * q : 32 * q + 4, :].bitcast(I32),
                     in_=scales[0, 4 * q : 4 * q + 4, :].bitcast(I32),
@@ -88,17 +88,17 @@ def tile_list_middle_of_three_kernel(
             )
             nc.scalar.copy(out=z[:, at : at + T], in_=bank[:])
 
-        def first_product():
-            at = place_b[0]
+        def early_product_b(i):
+            at = place_b[i]
             half = T // 2
-            for h, copy in enumerate((nc.scalar.copy, nc.vector.tensor_copy)):
+            for s in (0, half):
                 bank = psum.tile([P, T], F32, name="bank")
                 nc.tensor.matmul_mx(
-                    out=bank[:, 0:half], lhsT=b_codes[0][:].bitcast(FP8X4), lhsT_scale=b_plane[0][:],
-                    rhs=x_codes[:, half * h : half * (h + 1)].bitcast(FP8X4),
-                    rhs_scale=x_plane[:, half * h : half * (h + 1)], start=True, stop=True,
+                    out=bank[:, 0:half], lhsT=b_codes[i][:].bitcast(FP8X4), lhsT_scale=b_plane[i][:],
+                    rhs=x_codes[:, s : s + half].bitcast(FP8X4),
+                    rhs_scale=x_plane[:, s : s + half], start=True, stop=True,
                 )
-                copy(out=zb[:, at + half * h : at + half * (h + 1)], in_=bank[:, 0:half])
+                nc.scalar.copy(out=zb[:, at + s : at + s + half], in_=bank[:, 0:half])
 
         def product_a(i):
             product(za, place_a[i], a_codes[:, 2 * P * i : 2 * P * (i + 1)].bitcast(FP4X4), a_plane[:, P * i : P * (i + 1)])
@@ -131,7 +131,7 @@ def tile_list_middle_of_three_kernel(
 
         load_b(0)
         nc.sync.dma_start(out=x_codes[:].bitcast(I32), in_=xt_words[0].rearrange("p n t -> p (n t)").bitcast(I32))
-        load_plane(x_plane, xt_scales, nc.scalar)
+        load_plane(x_plane, xt_scales, (nc.sync, nc.scalar) * 2)
         nc.scalar.copy(out=za[:, TILES * T :], in_=zb[:, TILES * T :])
         nc.scalar.copy(out=zc[:, TILES * T :], in_=zb[:, TILES * T :])
         load_b(1)
@@ -148,8 +148,8 @@ def tile_list_middle_of_three_kernel(
         quantize_b(0)
         nc.vector.tensor_copy(out=b_grouped[1][:], in_=b_raw[1][:].rearrange("p j n -> p n j"))
         quantize_b(1)
-        first_product()
-        product_b(1)
+        early_product_b(0)
+        early_product_b(1)
         product_a(0)
         product_a(1)
         nc.scalar.copy(out=b_grouped[2][:], in_=b_raw[2][:].rearrange("p j n -> p n j"))

@@ -19,7 +19,12 @@ MAX = mybir.AluOpType.max
 P = 128
 PACK = 4
 TILES = N // P
+BANKS = 8
 SPARE = 192
+PIECES = [(0, P), (P, 2 * P), (2 * P, N)]
+PLACE_A = [3 * T, T, 2 * T, 0]
+PLACE_B = [3 * T, 2 * T, 0, T]
+PLACE_C = [2 * T, 3 * T, 0, T]
 
 
 def tile_list_middle_of_three_kernel(
@@ -28,7 +33,7 @@ def tile_list_middle_of_three_kernel(
     nc = tc.nc
     with ExitStack() as ctx:
         keep = ctx.enter_context(tc.tile_pool(name="keep", bufs=1))
-        psum = ctx.enter_context(tc.psum_pool(name="psum", bufs=8))
+        psum = ctx.enter_context(tc.psum_pool(name="psum", bufs=BANKS))
 
         list_a = keep.tile([P, J // 16], U16, name="list_a")
         list_b = keep.tile([P, J // 16], U16, name="list_b")
@@ -40,29 +45,28 @@ def tile_list_middle_of_three_kernel(
         c_codes = keep.tile([P, N], U32, name="c_codes", align_bytes=64)
         c_plane = keep.tile([P, N], U8, name="c_plane", align_bytes=64)
 
-        pieces = [(0, 128), (128, 256), (256, 512)]
-        b_raw = [keep.tile([P, PACK, e - s], F32, name="b_raw%d" % s) for s, e in pieces]
-        b_grouped = [keep.tile([P, e - s, PACK], BF16, name="b_grouped%d" % s, align_bytes=64) for s, e in pieces]
-        b_codes = [keep.tile([P, e - s], U32, name="b_codes%d" % s, align_bytes=64) for s, e in pieces]
-        b_plane = [keep.tile([P, e - s], U8, name="b_plane%d" % s, align_bytes=64) for s, e in pieces]
+        b_raw = [keep.tile([P, PACK, e - s], F32, name="b_raw%d" % s) for s, e in PIECES]
+        b_grouped = [keep.tile([P, e - s, PACK], BF16, name="b_grouped%d" % s, align_bytes=64) for s, e in PIECES]
+        b_codes = [keep.tile([P, e - s], U32, name="b_codes%d" % s, align_bytes=64) for s, e in PIECES]
+        b_plane = [keep.tile([P, e - s], U8, name="b_plane%d" % s, align_bytes=64) for s, e in PIECES]
 
         za = keep.tile([P, TILES * T + SPARE], F32, name="za")
         zb = keep.tile([P, TILES * T + SPARE], F32, name="zb")
         zc = keep.tile([P, TILES * T + SPARE], F32, name="zc")
-        place_a = [3 * T, 2 * T, 0, T]
-        place_b = [3 * T, 2 * T, 0, T]
-        place_c = [2 * T, 3 * T, 0, T]
-        ga = [keep.tile([P, J], F32, name="ga%d" % i) for i in range(TILES)]
-        gb = [keep.tile([P, J], F32, name="gb%d" % i) for i in range(TILES)]
-        gc = [keep.tile([P, J], F32, name="gc%d" % i) for i in range(TILES)]
-        lo = [keep.tile([P, J], F32, name="lo%d" % i) for i in range(TILES)]
-        hi = [keep.tile([P, J], F32, name="hi%d" % i) for i in range(TILES)]
-        capped = [keep.tile([P, J], F32, name="capped%d" % i) for i in range(TILES)]
-        middle = [keep.tile([P, J], F32, name="middle%d" % i) for i in range(TILES)]
+        ga = keep.tile([P, TILES * J], F32, name="ga")
+        gb = keep.tile([P, TILES * J], F32, name="gb")
+        gc = keep.tile([P, TILES * J], F32, name="gc")
+        lo = keep.tile([P, TILES * J], F32, name="lo")
+        hi = keep.tile([P, TILES * J], F32, name="hi")
+        capped = keep.tile([P, TILES * J], F32, name="capped")
+        middle = keep.tile([P, TILES * J], F32, name="middle")
 
-        wb_rows = wb.rearrange("(p j) n -> p j n", j=PACK)
+        wb_rows = wb.rearrange("(p t) n -> p t n", t=PACK)
 
-        def load_plane(plane, scales, queues=(nc.sync,) * 4):
+        def load_e4m3_words(codes, words):
+            nc.sync.dma_start(out=codes[:].bitcast(I32), in_=words[0].rearrange("p n t -> p (n t)").bitcast(I32))
+
+        def load_plane(plane, scales, queues):
             for q, queue in enumerate(queues):
                 queue.dma_start(
                     out=plane[32 * q : 32 * q + 4, :].bitcast(I32),
@@ -70,120 +74,127 @@ def tile_list_middle_of_three_kernel(
                 )
 
         def load_b(u):
-            s, e = pieces[u]
+            s, e = PIECES[u]
             nc.sync.dma_start(out=b_raw[u][:], in_=wb_rows[:, :, s:e])
+
+        def round_b(u, copy):
+            copy(out=b_grouped[u][:], in_=b_raw[u][:].rearrange("p t n -> p n t"))
 
         def quantize_b(u):
             nc.vector.quantize_mx(
                 out=b_codes[u][:].bitcast(FP8X4),
                 scales=b_plane[u][:],
-                in_=b_grouped[u][:].rearrange("p n j -> p (n j)"),
+                in_=b_grouped[u][:].rearrange("p n t -> p (n t)"),
             )
 
-        def product(z, at, codes, plane):
-            bank = psum.tile([P, T], F32, name="bank")
-            nc.tensor.matmul_mx(
-                out=bank[:], lhsT=codes, lhsT_scale=plane,
-                rhs=x_codes[:].bitcast(FP8X4), rhs_scale=x_plane[:], start=True, stop=True,
-            )
-            nc.scalar.copy(out=z[:, at : at + T], in_=bank[:])
-
-        def early_product_b(i):
-            at = place_b[i]
-            half = T // 2
-            for s in (0, half):
+        def product(z, at, codes, plane, width=T):
+            for s in range(0, T, width):
                 bank = psum.tile([P, T], F32, name="bank")
                 nc.tensor.matmul_mx(
-                    out=bank[:, 0:half], lhsT=b_codes[i][:].bitcast(FP8X4), lhsT_scale=b_plane[i][:],
-                    rhs=x_codes[:, s : s + half].bitcast(FP8X4),
-                    rhs_scale=x_plane[:, s : s + half], start=True, stop=True,
+                    out=bank[:, 0:width],
+                    lhsT=codes,
+                    lhsT_scale=plane,
+                    rhs=x_codes[:, s : s + width].bitcast(FP8X4),
+                    rhs_scale=x_plane[:, s : s + width],
+                    start=True,
+                    stop=True,
                 )
-                nc.scalar.copy(out=zb[:, at + s : at + s + half], in_=bank[:, 0:half])
+                nc.scalar.copy(out=z[:, at + s : at + s + width], in_=bank[:, 0:width])
 
         def product_a(i):
-            product(za, place_a[i], a_codes[:, 2 * P * i : 2 * P * (i + 1)].bitcast(FP4X4), a_plane[:, P * i : P * (i + 1)])
+            codes = a_codes[:, 2 * P * i : 2 * P * (i + 1)].bitcast(FP4X4)
+            product(za, PLACE_A[i], codes, a_plane[:, P * i : P * (i + 1)])
 
-        def product_b(i):
-            u = min(i, 2)
-            s = P * i - pieces[u][0]
-            product(zb, place_b[i], b_codes[u][:, s : s + P].bitcast(FP8X4), b_plane[u][:, s : s + P])
+        def product_b(i, width=T):
+            u = min(i, len(PIECES) - 1)
+            s = P * i - PIECES[u][0]
+            product(zb, PLACE_B[i], b_codes[u][:, s : s + P].bitcast(FP8X4), b_plane[u][:, s : s + P], width)
 
         def product_c(i):
-            product(zc, place_c[i], c_codes[:, P * i : P * (i + 1)].bitcast(FP8X4), c_plane[:, P * i : P * (i + 1)])
+            product(zc, PLACE_C[i], c_codes[:, P * i : P * (i + 1)].bitcast(FP8X4), c_plane[:, P * i : P * (i + 1)])
 
         def gather(g, z, place, offsets, i):
-            nc.vector.tensor_copy(out=g[i][:], in_=z[:, place[i] : place[i] + T + SPARE].indirect(offsets[:]))
+            window = z[:, place[i] : place[i] + T + SPARE]
+            nc.vector.tensor_copy(out=g[:, J * i : J * (i + 1)], in_=window.indirect(offsets[:]))
 
-        def bounds(i):
-            nc.vector.tensor_tensor(out=lo[i][:], in0=ga[i][:], in1=gb[i][:], op=MIN)
-            nc.vector.tensor_tensor(out=hi[i][:], in0=ga[i][:], in1=gb[i][:], op=MAX)
+        def gather_a(i):
+            gather(ga, za, PLACE_A, list_a, i)
 
-        def cap(i, cols=slice(0, J)):
-            nc.vector.tensor_tensor(out=capped[i][:, cols], in0=hi[i][:, cols], in1=gc[i][:, cols], op=MIN)
+        def gather_b(i):
+            gather(gb, zb, PLACE_B, list_b, i)
 
-        def finish(i, cols=slice(0, J), queue=nc.sync):
-            nc.vector.tensor_tensor(out=middle[i][:, cols], in0=lo[i][:, cols], in1=capped[i][:, cols], op=MAX)
-            queue.dma_start(out=out[P * i : P * (i + 1), cols], in_=middle[i][:, cols])
+        def gather_c(i):
+            gather(gc, zc, PLACE_C, list_c, i)
+
+        def bounds(s, e):
+            nc.vector.tensor_tensor(out=lo[:, s:e], in0=ga[:, s:e], in1=gb[:, s:e], op=MIN)
+            nc.vector.tensor_tensor(out=hi[:, s:e], in0=ga[:, s:e], in1=gb[:, s:e], op=MAX)
+
+        def cap(s, e):
+            nc.vector.tensor_tensor(out=capped[:, s:e], in0=hi[:, s:e], in1=gc[:, s:e], op=MIN)
+
+        def finish(s, e, queue=nc.sync):
+            nc.vector.tensor_tensor(out=middle[:, s:e], in0=lo[:, s:e], in1=capped[:, s:e], op=MAX)
+            i = s // J
+            queue.dma_start(out=out[P * i : P * (i + 1), s - J * i : e - J * i], in_=middle[:, s:e])
 
         for plane in (x_plane, a_plane, c_plane):
             nc.vector.memset(plane[:].bitcast(I32), 0)
         nc.vector.memset(zb[:, TILES * T :], 0.0)
 
         load_b(0)
-        nc.sync.dma_start(out=x_codes[:].bitcast(I32), in_=xt_words[0].rearrange("p n t -> p (n t)").bitcast(I32))
+        load_e4m3_words(x_codes, xt_words)
         load_plane(x_plane, xt_scales, (nc.sync, nc.scalar) * 2)
         nc.scalar.copy(out=za[:, TILES * T :], in_=zb[:, TILES * T :])
         nc.scalar.copy(out=zc[:, TILES * T :], in_=zb[:, TILES * T :])
         load_b(1)
         nc.sync.dma_start(list_b[:], offs2)
         nc.sync.dma_start(out=a_codes[:].bitcast(I32), in_=wa_words[0].bitcast(I32))
-        load_plane(a_plane, wa_scales)
+        load_plane(a_plane, wa_scales, (nc.sync,) * 4)
         nc.sync.dma_start(list_a[:], offs)
         load_b(2)
-        nc.sync.dma_start(out=c_codes[:].bitcast(I32), in_=wc_words[0].rearrange("p n t -> p (n t)").bitcast(I32))
-        load_plane(c_plane, wc_scales)
+        load_e4m3_words(c_codes, wc_words)
+        load_plane(c_plane, wc_scales, (nc.sync,) * 4)
         nc.sync.dma_start(list_c[:], offs3)
 
-        nc.vector.tensor_copy(out=b_grouped[0][:], in_=b_raw[0][:].rearrange("p j n -> p n j"))
-        quantize_b(0)
-        nc.vector.tensor_copy(out=b_grouped[1][:], in_=b_raw[1][:].rearrange("p j n -> p n j"))
-        quantize_b(1)
-        early_product_b(0)
-        early_product_b(1)
-        product_a(0)
-        product_a(1)
-        nc.scalar.copy(out=b_grouped[2][:], in_=b_raw[2][:].rearrange("p j n -> p n j"))
-        gather(gb, zb, place_b, list_b, 0)
-        gather(gb, zb, place_b, list_b, 1)
-        gather(ga, za, place_a, list_a, 0)
-        gather(ga, za, place_a, list_a, 1)
-        quantize_b(2)
-        for i in (2, 3):
+        for u in (0, 1):
+            round_b(u, nc.vector.tensor_copy)
+            quantize_b(u)
+        for i in (0, 1):
+            product_b(i, T // 2)
+
+        for i in (0, 1, 2):
             product_a(i)
+        round_b(2, nc.scalar.copy)
+        for i in (0, 1):
+            gather_b(i)
+        for i in (0, 1, 2):
+            gather_a(i)
+        quantize_b(2)
+        product_a(3)
+        for i in (0, 1):
+            product_c(i)
         for i in (2, 3):
             product_b(i)
-        for i in range(TILES):
+        for i in (2, 3):
             product_c(i)
-        bounds(0)
-        bounds(1)
+
+        bounds(0, 2 * J)
+        gather_a(3)
+        for i in (0, 1):
+            gather_c(i)
         for i in (2, 3):
-            gather(ga, za, place_a, list_a, i)
-        for i in (2, 3):
-            gather(gb, zb, place_b, list_b, i)
-        bounds(2)
-        bounds(3)
-        gather(gc, zc, place_c, list_c, 0)
-        gather(gc, zc, place_c, list_c, 1)
-        cap(0)
-        gather(gc, zc, place_c, list_c, 2)
-        finish(0)
-        cap(1)
-        cap(2)
-        finish(1)
-        gather(gc, zc, place_c, list_c, 3)
-        finish(2)
-        halves = (slice(0, J // 2), slice(J // 2, J))
-        for cols in halves:
-            cap(3, cols)
-        finish(3, halves[0], nc.scalar)
-        finish(3, halves[1], nc.sync)
+            gather_b(i)
+        cap(0, 2 * J)
+        bounds(2 * J, 4 * J)
+        for i in (0, 1):
+            finish(J * i, J * (i + 1))
+            gather_c(i + 2)
+
+        half = 3 * J + J // 2
+        cap(2 * J, 3 * J)
+        cap(3 * J, half)
+        finish(2 * J, 3 * J)
+        cap(half, 4 * J)
+        finish(3 * J, half, nc.scalar)
+        finish(half, 4 * J)

from contextlib import ExitStack

import concourse.mybir as mybir

K, T, J, N = 512, 512, 512, 512
FLOPS = 3 * 2 * K * T * N

F32 = mybir.dt.float32
BF16 = mybir.dt.bfloat16
I32 = mybir.dt.int32
U32 = mybir.dt.uint32
U16 = mybir.dt.uint16
U8 = mybir.dt.uint8
FP8X4 = mybir.dt.float8_e4m3fn_x4
FP4X4 = mybir.dt.float4_e2m1fn_x4
MIN = mybir.AluOpType.min
MAX = mybir.AluOpType.max

P = 128
PACK = 4
TILES = N // P
BANKS = 8
SPARE = 192
PIECES = [(0, P), (P, 2 * P), (2 * P, N)]
PLACE_A = [3 * T, T, 2 * T, 0]
PLACE_B = [3 * T, 2 * T, 0, T]
PLACE_C = [2 * T, 3 * T, 0, T]


def tile_list_middle_of_three_kernel(
    tc, xt_words, xt_scales, wa_words, wa_scales, wb, wc_words, wc_scales, offs, offs2, offs3, out
):
    nc = tc.nc
    with ExitStack() as ctx:
        keep = ctx.enter_context(tc.tile_pool(name="keep", bufs=1))
        psum = ctx.enter_context(tc.psum_pool(name="psum", bufs=BANKS))

        list_a = keep.tile([P, J // 16], U16, name="list_a")
        list_b = keep.tile([P, J // 16], U16, name="list_b")
        list_c = keep.tile([P, J // 16], U16, name="list_c")
        x_codes = keep.tile([P, T], U32, name="x_codes", align_bytes=64)
        x_plane = keep.tile([P, T], U8, name="x_plane", align_bytes=64)
        a_codes = keep.tile([P, 2 * N], U8, name="a_codes", align_bytes=64)
        a_plane = keep.tile([P, N], U8, name="a_plane", align_bytes=64)
        c_codes = keep.tile([P, N], U32, name="c_codes", align_bytes=64)
        c_plane = keep.tile([P, N], U8, name="c_plane", align_bytes=64)

        b_raw = [keep.tile([P, PACK, e - s], F32, name="b_raw%d" % s) for s, e in PIECES]
        b_grouped = [keep.tile([P, e - s, PACK], BF16, name="b_grouped%d" % s, align_bytes=64) for s, e in PIECES]
        b_codes = [keep.tile([P, e - s], U32, name="b_codes%d" % s, align_bytes=64) for s, e in PIECES]
        b_plane = [keep.tile([P, e - s], U8, name="b_plane%d" % s, align_bytes=64) for s, e in PIECES]

        za = keep.tile([P, TILES * T + SPARE], F32, name="za")
        zb = keep.tile([P, TILES * T + SPARE], F32, name="zb")
        zc = keep.tile([P, TILES * T + SPARE], F32, name="zc")
        ga = keep.tile([P, TILES * J], F32, name="ga")
        gb = keep.tile([P, TILES * J], F32, name="gb")
        gc = keep.tile([P, TILES * J], F32, name="gc")
        lo = keep.tile([P, TILES * J], F32, name="lo")
        hi = keep.tile([P, TILES * J], F32, name="hi")
        capped = keep.tile([P, TILES * J], F32, name="capped")
        middle = keep.tile([P, TILES * J], F32, name="middle")

        wb_rows = wb.rearrange("(p t) n -> p t n", t=PACK)

        def load_e4m3_words(codes, words):
            nc.sync.dma_start(out=codes[:].bitcast(I32), in_=words[0].rearrange("p n t -> p (n t)").bitcast(I32))

        def load_plane(plane, scales, queues):
            for q, queue in enumerate(queues):
                queue.dma_start(
                    out=plane[32 * q : 32 * q + 4, :].bitcast(I32),
                    in_=scales[0, 4 * q : 4 * q + 4, :].bitcast(I32),
                )

        def load_b(u):
            s, e = PIECES[u]
            nc.sync.dma_start(out=b_raw[u][:], in_=wb_rows[:, :, s:e])

        def round_b(u, copy):
            copy(out=b_grouped[u][:], in_=b_raw[u][:].rearrange("p t n -> p n t"))

        def quantize_b(u):
            nc.vector.quantize_mx(
                out=b_codes[u][:].bitcast(FP8X4),
                scales=b_plane[u][:],
                in_=b_grouped[u][:].rearrange("p n t -> p (n t)"),
            )

        def product(z, at, codes, plane, width=T):
            for s in range(0, T, width):
                bank = psum.tile([P, T], F32, name="bank")
                nc.tensor.matmul_mx(
                    out=bank[:, 0:width],
                    lhsT=codes,
                    lhsT_scale=plane,
                    rhs=x_codes[:, s : s + width].bitcast(FP8X4),
                    rhs_scale=x_plane[:, s : s + width],
                    start=True,
                    stop=True,
                )
                nc.scalar.copy(out=z[:, at + s : at + s + width], in_=bank[:, 0:width])

        def product_a(i):
            codes = a_codes[:, 2 * P * i : 2 * P * (i + 1)].bitcast(FP4X4)
            product(za, PLACE_A[i], codes, a_plane[:, P * i : P * (i + 1)])

        def product_b(i, width=T):
            u = min(i, len(PIECES) - 1)
            s = P * i - PIECES[u][0]
            product(zb, PLACE_B[i], b_codes[u][:, s : s + P].bitcast(FP8X4), b_plane[u][:, s : s + P], width)

        def product_c(i):
            product(zc, PLACE_C[i], c_codes[:, P * i : P * (i + 1)].bitcast(FP8X4), c_plane[:, P * i : P * (i + 1)])

        def gather(g, z, place, offsets, i):
            window = z[:, place[i] : place[i] + T + SPARE]
            nc.vector.tensor_copy(out=g[:, J * i : J * (i + 1)], in_=window.indirect(offsets[:]))

        def gather_a(i):
            gather(ga, za, PLACE_A, list_a, i)

        def gather_b(i):
            gather(gb, zb, PLACE_B, list_b, i)

        def gather_c(i):
            gather(gc, zc, PLACE_C, list_c, i)

        def bounds(s, e):
            nc.vector.tensor_tensor(out=lo[:, s:e], in0=ga[:, s:e], in1=gb[:, s:e], op=MIN)
            nc.vector.tensor_tensor(out=hi[:, s:e], in0=ga[:, s:e], in1=gb[:, s:e], op=MAX)

        def cap(s, e):
            nc.vector.tensor_tensor(out=capped[:, s:e], in0=hi[:, s:e], in1=gc[:, s:e], op=MIN)

        def finish(s, e, queue=nc.sync):
            nc.vector.tensor_tensor(out=middle[:, s:e], in0=lo[:, s:e], in1=capped[:, s:e], op=MAX)
            i = s // J
            queue.dma_start(out=out[P * i : P * (i + 1), s - J * i : e - J * i], in_=middle[:, s:e])

        for plane in (x_plane, a_plane, c_plane):
            nc.vector.memset(plane[:].bitcast(I32), 0)
        nc.vector.memset(zb[:, TILES * T :], 0.0)

        load_b(0)
        load_e4m3_words(x_codes, xt_words)
        load_plane(x_plane, xt_scales, (nc.sync, nc.scalar) * 2)
        nc.scalar.copy(out=za[:, TILES * T :], in_=zb[:, TILES * T :])
        nc.scalar.copy(out=zc[:, TILES * T :], in_=zb[:, TILES * T :])
        load_b(1)
        nc.sync.dma_start(list_b[:], offs2)
        nc.sync.dma_start(out=a_codes[:].bitcast(I32), in_=wa_words[0].bitcast(I32))
        load_plane(a_plane, wa_scales, (nc.sync,) * 4)
        nc.sync.dma_start(list_a[:], offs)
        load_b(2)
        load_e4m3_words(c_codes, wc_words)
        load_plane(c_plane, wc_scales, (nc.sync,) * 4)
        nc.sync.dma_start(list_c[:], offs3)

        for u in (0, 1):
            round_b(u, nc.vector.tensor_copy)
            quantize_b(u)
        for i in (0, 1):
            product_b(i, T // 2)

        for i in (0, 1, 2):
            product_a(i)
        round_b(2, nc.scalar.copy)
        for i in (0, 1):
            gather_b(i)
        for i in (0, 1, 2):
            gather_a(i)
        quantize_b(2)
        product_a(3)
        for i in (0, 1):
            product_c(i)
        for i in (2, 3):
            product_b(i)
        for i in (2, 3):
            product_c(i)

        bounds(0, 2 * J)
        gather_a(3)
        for i in (0, 1):
            gather_c(i)
        for i in (2, 3):
            gather_b(i)
        cap(0, 2 * J)
        bounds(2 * J, 4 * J)
        for i in (0, 1):
            finish(J * i, J * (i + 1))
            gather_c(i + 2)

        half = 3 * J + J // 2
        cap(2 * J, 3 * J)
        cap(3 * J, half)
        finish(2 * J, 3 * J)
        cap(half, 4 * J)
        finish(3 * J, half, nc.scalar)
        finish(half, 4 * J)
